import numpy as np
import ml_dtypes


def mxq(x, axis, fmt="e4m3"):
    dtype, down = {"e4m3": (ml_dtypes.float8_e4m3fn, 7), "e5m2": (ml_dtypes.float8_e5m2, 14)}[fmt]
    v = np.moveaxis(np.asarray(x, np.float32).astype(ml_dtypes.bfloat16).astype(np.float64), axis, -1)
    blocks = v.reshape(v.shape[:-1] + (-1, 32))
    amax = np.abs(blocks).max(-1, keepdims=True)
    byte = np.maximum(np.where(amax > 0, np.frexp(amax)[1] - 1 + 127, 0) - down, 1)
    scale = np.exp2(byte - 127.0)
    codes = (blocks / scale).astype(np.float32).astype(dtype).astype(np.float64)
    return np.moveaxis((codes * scale).reshape(v.shape), -1, axis)


WIDE = False


def mx_kscale(k):
    if not WIDE:
        return np.ones(k)
    levels = np.array([30, -30])
    if k % 512:
        return np.exp2(np.random.permutation(np.resize(levels, k // 32))).repeat(32)
    a = np.empty((k // 512, 16))
    for p in range(k // 512):
        a[p, :8] = np.random.permutation(np.resize(levels, 8))
        for g in range(8):
            far = levels[np.abs(levels - a[p, g]) >= 10]
            a[p, g + 8] = far[np.random.randint(len(far))]
    return np.exp2(a.ravel()).repeat(32)


def f64(x):
    return np.asarray(x).astype(np.float64)


def striped(idx):
    return np.tile(np.asarray(idx).reshape(-1, 16).T, (8, 1)).astype(np.uint16)


def unstriped(offs):
    return offs[:16].T.reshape(-1).astype(np.int64)


E2M1 = np.array([0.0, 0.5, 1.0, 1.5, 2.0, 3.0, 4.0, 6.0, -0.0, -0.5, -1.0, -1.5, -2.0, -3.0, -4.0, -6.0])


def pack_weight(w, fmt):
    k, n = w.shape
    w = f64(np.asarray(w, np.float32).astype(ml_dtypes.bfloat16)).reshape(k // 32, 32, n)
    amax = np.abs(w).max(1)
    if fmt in ("e4m3", "e5m2"):
        byte = np.frexp(amax)[1] - 1 + 127 - (7 if fmt == "e4m3" else 14)
    else:
        mant, ex = np.frexp(amax / 6.0)
        byte = np.where(mant > 0.5, ex, ex - 1) + 127
    byte = np.clip(np.where(amax > 0, byte, 1), 1, 254)
    scaled = (w * np.exp2(127.0 - byte)[:, None, :]).reshape(k, n).astype(np.float32)
    by_word = np.ascontiguousarray(scaled.reshape(k // 512, 128, 4, n).transpose(0, 1, 3, 2))
    if fmt in ("e4m3", "e5m2"):
        words = by_word.astype(ml_dtypes.float8_e4m3fn if fmt == "e4m3" else ml_dtypes.float8_e5m2).view(np.uint8)
    else:
        c = by_word.astype(ml_dtypes.float4_e2m1fn).view(np.uint8) & 0xF
        words = (c[..., 0::2] | (c[..., 1::2] << 4)).reshape(k // 512, 128, 2 * n)
    return np.ascontiguousarray(words), np.ascontiguousarray(byte.astype(np.uint8).reshape(k // 512, 16, n))


def unpack_weight(words, scales, fmt):
    g, _, n = scales.shape
    words = np.ascontiguousarray(words).reshape(g, 128, n, -1)
    if fmt in ("e4m3", "e5m2"):
        vals = words.view(ml_dtypes.float8_e4m3fn if fmt == "e4m3" else ml_dtypes.float8_e5m2).astype(np.float64)
    else:
        nib = np.empty((g, 128, n, 4), np.uint8)
        nib[..., 0::2] = words & 0xF
        nib[..., 1::2] = words >> 4
        vals = E2M1[nib]
    vals = vals * np.repeat(np.exp2(scales.astype(np.float64) - 127.0), 8, axis=1)[..., None]
    return vals.transpose(0, 1, 3, 2).reshape(g * 512, n)


K, F, T, Z, J, R, O, N, E = 512, 512, 1024, 1024, 256, 512, 128, 256, 1024


def setup_inputs():
    n = np.random.standard_normal
    idx = np.random.permutation(T)[:J]
    idx2 = np.random.permutation(Z)[:J]
    idx3 = np.random.permutation(J)[:O]
    idx4 = np.random.permutation(T)[:O]
    idx5 = np.random.permutation(E)[:O]
    fk = mx_kscale(K)
    fr = mx_kscale(R)
    ff = mx_kscale(F)
    xtp = pack_weight(n((K, T)) / fk[:, None], "e5m2")
    wp = pack_weight(n((K, R)) * 1 / np.sqrt(K) * fk[:, None] * fr, "e2m1")
    xop = pack_weight(n((F, Z)) / ff[:, None], "e4m3")
    w2p = pack_weight(n((F, R)) * 1 / np.sqrt(F) * ff[:, None] * fr, "e2m1")
    wbp = pack_weight(n((R, N)) * 1 / np.sqrt(R) / fr[:, None], "e2m1")
    wsp = pack_weight(n((K, N)) * 1 / np.sqrt(K) * fk[:, None], "e2m1")
    return {
        "xt_words": xtp[0],
        "xt_scales": xtp[1],
        "w_words": wp[0],
        "w_scales": wp[1],
        "xo_words": xop[0],
        "xo_scales": xop[1],
        "w2_words": w2p[0],
        "w2_scales": w2p[1],
        "sa": (np.random.uniform(0.5, 1.6, (R, 1))).astype(np.float32),
        "wb_words": wbp[0],
        "wb_scales": wbp[1],
        "ws_words": wsp[0],
        "ws_scales": wsp[1],
        "tz": (np.random.randint(-9, 10, (N, E)).astype(np.float64)).astype(np.float32),
        "so": (np.random.uniform(0.1, 0.3, (N, 1))).astype(np.float32),
        "offs": striped(idx),
        "offs2": striped(idx2),
        "offs3": striped(idx3),
        "offs4": striped(idx4),
        "offs5": striped(idx5),
    }


def reference(xt_words, xt_scales, w_words, w_scales, xo_words, xo_scales, w2_words, w2_scales, sa, wb_words, wb_scales, ws_words, ws_scales, tz, so, offs, offs2, offs3, offs4, offs5):
    idx = unstriped(offs)
    idx2 = unstriped(offs2)
    idx3 = unstriped(offs3)
    idx4 = unstriped(offs4)
    idx5 = unstriped(offs5)
    xtu = unpack_weight(xt_words, xt_scales, "e5m2")
    wu = unpack_weight(w_words, w_scales, "e2m1")
    xou = unpack_weight(xo_words, xo_scales, "e4m3")
    w2u = unpack_weight(w2_words, w2_scales, "e2m1")
    wbu = unpack_weight(wb_words, wb_scales, "e2m1")
    wsu = unpack_weight(ws_words, ws_scales, "e2m1")
    xtidxg = xtu[:, idx]
    a = wu.T @ xtidxg
    xoidx2g = xou[:, idx2]
    b = w2u.T @ xoidx2g
    g1 = np.maximum(a, b)
    hid = g1[:, idx3] * f64(sa)
    hidq = mxq(hid, 0, "e4m3")
    xtidx4g = xtu[:, idx4]
    p = wbu.T @ hidq + wsu.T @ xtidx4g
    y = np.maximum(p, f64(tz)[:, idx5] * f64(so))
    return y

@@ -1,0 +1,166 @@
+from contextlib import ExitStack
+
+import concourse.mybir as mybir
+
+K, T, J, R, O, N, E = 512, 1024, 256, 512, 128, 256, 1024
+FLOPS = 2 * K * R * J * 2 + 2 * R * N * O * 2
+
+F32 = mybir.dt.float32
+BF16 = mybir.dt.bfloat16
+I32 = mybir.dt.int32
+U32 = mybir.dt.uint32
+U16 = mybir.dt.uint16
+U8 = mybir.dt.uint8
+E4M3 = mybir.dt.float8_e4m3fn_x4
+E5M2 = mybir.dt.float8_e5m2_x4
+E2M1 = mybir.dt.float4_e2m1fn_x4
+COPY = mybir.ActivationFunctionType.Copy
+MAX = mybir.AluOpType.max
+
+P = 128
+PACK = 4
+QUADS = 4
+QROWS = 32
+
+
+def tile_list_largestpicked_twotab_further_stepfloor_kernel(
+    tc, xt_words, xt_scales, w_words, w_scales, xo_words, xo_scales, w2_words, w2_scales, sa,
+    wb_words, wb_scales, ws_words, ws_scales, tz, so, offs, offs2, offs3, offs4, offs5, out,
+):
+    nc = tc.nc
+    with ExitStack() as ctx:
+        lists = ctx.enter_context(tc.tile_pool(name="lists", bufs=1))
+        sb = ctx.enter_context(tc.tile_pool(name="sb", bufs=1))
+        ps = ctx.enter_context(tc.psum_pool(name="ps", bufs=1))
+
+        def tile(shape, dtype, name):
+            return sb.tile(shape, dtype, name=name, align_bytes=64)
+
+        def load_list(src, name):
+            t = lists.tile(list(src.shape), U16, name=name)
+            nc.sync.dma_start(t[:], src)
+            return t
+
+        def load_plane(engine, plane, scales):
+            rows = scales[0].bitcast(I32)
+            for q in range(QUADS):
+                engine.dma_start(plane[QROWS * q : QROWS * q + PACK, :].bitcast(I32), rows[PACK * q : PACK * (q + 1), :])
+
+        xt_plane = tile([P, T], U8, "xt_plane")
+        xo_plane = tile([P, T], U8, "xo_plane")
+        w_plane = tile([P, 2 * R], U8, "w_plane")
+        ws_plane = tile([P, N], U8, "ws_plane")
+        wb_plane = tile([P, N], U8, "wb_plane")
+        for plane in (xt_plane, xo_plane, w_plane, ws_plane, wb_plane):
+            nc.vector.memset(plane[:].bitcast(I32), 0)
+
+        w_stage = tile([PACK, QUADS, 2 * R // 4], I32, "w_stage")
+        for i, scales in enumerate((w_scales, w2_scales)):
+            nc.sync.dma_start(
+                w_stage[:, :, i * R // 4 : (i + 1) * R // 4],
+                scales[0].bitcast(I32).rearrange("(q r) c -> r q c", r=PACK),
+            )
+        idx = load_list(offs, "idx")
+        load_plane(nc.scalar, xt_plane, xt_scales)
+        xt_tab = tile([P, T], U32, "xt_tab")
+        nc.sync.dma_start(xt_tab[:].bitcast(I32), xt_words[0].rearrange("p c r -> p (c r)").bitcast(I32))
+        w_raw = tile([P, R], U16, "w_raw")
+        nc.sync.dma_start(w_raw[:].bitcast(I32), w_words[0].bitcast(I32))
+        w2_raw = tile([P, R], U16, "w2_raw")
+        nc.sync.dma_start(w2_raw[:].bitcast(I32), w2_words[0].bitcast(I32))
+        xo_tab = tile([P, T], U32, "xo_tab")
+        nc.sync.dma_start(xo_tab[:].bitcast(I32), xo_words[0].rearrange("p c r -> p (c r)").bitcast(I32))
+        idx2 = load_list(offs2, "idx2")
+        load_plane(nc.sync, xo_plane, xo_scales)
+        tz_rows = [tile([P, E], F32, "tz_rows%d" % h) for h in range(2)]
+        idx4 = load_list(offs4, "idx4")
+        nc.sync.dma_start(tz_rows[0][:], tz[0:P, :])
+        idx3 = load_list(offs3, "idx3")
+        nc.sync.dma_start(tz_rows[1][:], tz[P : 2 * P, :])
+        idx5 = load_list(offs5, "idx5")
+        load_plane(nc.sync, ws_plane, ws_scales)
+        load_plane(nc.sync, wb_plane, wb_scales)
+
+        sa_cols = tile([P, PACK], F32, "sa_cols")
+        nc.gpsimd.dma_start(sa_cols[:], sa.rearrange("(p t) o -> p (t o)", t=PACK))
+        so_cols = tile([P, 2], F32, "so_cols")
+        with nc.allow_non_contiguous_dma(reason="one step a partition"):
+            nc.gpsimd.dma_start(so_cols[:], so.rearrange("(h p) o -> p (h o)", p=P))
+        ws_codes = tile([P, N], U16, "ws_codes")
+        nc.gpsimd.dma_start(ws_codes[:].bitcast(I32), ws_words[0].bitcast(I32))
+        wb_codes = tile([P, N], U16, "wb_codes")
+        nc.gpsimd.dma_start(wb_codes[:].bitcast(I32), wb_words[0].bitcast(I32))
+
+        for q in range(QUADS):
+            nc.vector.tensor_copy(w_plane[QROWS * q : QROWS * q + PACK, :].bitcast(I32), w_stage[:, q, :])
+
+        def gather(tab, plane, offsets, count, name):
+            scales = tile([P, count], U8, name + "_scales")
+            nc.vector.tensor_copy(scales[:], plane[:].indirect(offsets[:]))
+            codes = tile([P, count], U32, name + "_codes")
+            nc.vector.tensor_copy(codes[:], tab[:].indirect(offsets[:]))
+            return codes, scales
+
+        def deal(raw, plane, name):
+            codes = tile([P, PACK, P], U16, name + "_codes")
+            nc.scalar.copy(codes[:], raw[:].rearrange("p (m t) -> p t m", t=PACK))
+            scales = tile([P, PACK, P], U8, name + "_scales")
+            nc.vector.tensor_copy(scales[:], plane.rearrange("p (m t) -> p t m", t=PACK))
+            return codes, scales
+
+        xa_codes, xa_scales = gather(xt_tab, xt_plane, idx, J, "xa")
+        w_codes, w_sc = deal(w_raw, w_plane[:, 0:R], "w")
+        a_rows = tile([P, PACK, J], F32, "a_rows")
+        for pair in range(2):
+            a_bank = ps.tile([P, 2, J], F32, name="a_bank%d" % pair)
+            for u in range(2):
+                t = 2 * pair + u
+                nc.tensor.matmul_mx(
+                    out=a_bank[:, u, :], lhsT=w_codes[:, t, :].bitcast(E2M1), lhsT_scale=w_sc[:, t, :],
+                    rhs=xa_codes[:].bitcast(E5M2), rhs_scale=xa_scales[:], start=True, stop=True,
+                )
+            nc.scalar.copy(a_rows[:, 2 * pair : 2 * pair + 2, :], a_bank[:])
+
+        w2_codes, w2_sc = deal(w2_raw, w_plane[:, R : 2 * R], "w2")
+        xb_codes, xb_scales = gather(xo_tab, xo_plane, idx2, J, "xb")
+        xs_codes, xs_scales = gather(xt_tab, xt_plane, idx4, O, "xs")
+
+        hid = tile([P, PACK, O], BF16, "hid")
+        for t in range(PACK):
+            b_bank = ps.tile([P, J], F32, name="b_bank%d" % t)
+            nc.tensor.matmul_mx(
+                out=b_bank[:], lhsT=w2_codes[:, t, :].bitcast(E2M1), lhsT_scale=w2_sc[:, t, :],
+                rhs=xb_codes[:].bitcast(E4M3), rhs_scale=xb_scales[:], start=True, stop=True,
+            )
+            g1 = tile([P, J], F32, "g1_%d" % t)
+            nc.vector.tensor_tensor(g1[:], b_bank[:], a_rows[:, t, :], MAX)
+            nc.scalar.activation(hid[:, t, :], g1[:].indirect(idx3[:]), COPY, scale=sa_cols[:, t : t + 1])
+
+        p_banks = [ps.tile([P, O], F32, name="p_bank%d" % h) for h in range(2)]
+        floors = []
+        for h in range(2):
+            nc.tensor.matmul_mx(
+                out=p_banks[h][:], lhsT=ws_codes[:, P * h : P * (h + 1)].bitcast(E2M1),
+                lhsT_scale=ws_plane[:, P * h : P * (h + 1)],
+                rhs=xs_codes[:].bitcast(E5M2), rhs_scale=xs_scales[:], start=True, stop=False,
+            )
+            floor = tile([P, O], F32, "floor%d" % h)
+            nc.scalar.activation(floor[:], tz_rows[h][:].indirect(idx5[:]), COPY, scale=so_cols[:, h : h + 1])
+            floors.append(floor)
+
+        hid_woven = tile([P, O, PACK], BF16, "hid_woven")
+        nc.vector.tensor_copy(hid_woven[:], hid[:].rearrange("p t o -> p o t"))
+        hid_codes = tile([P, O], U32, "hid_codes")
+        hid_scales = tile([P, O], U8, "hid_scales")
+        nc.vector.quantize_mx(
+            out=hid_codes[:].bitcast(E4M3), scales=hid_scales[:], in_=hid_woven[:].rearrange("p o t -> p (o t)")
+        )
+        for h, queue in enumerate((nc.sync, nc.scalar)):
+            nc.tensor.matmul_mx(
+                out=p_banks[h][:], lhsT=wb_codes[:, P * h : P * (h + 1)].bitcast(E2M1),
+                lhsT_scale=wb_plane[:, P * h : P * (h + 1)],
+                rhs=hid_codes[:].bitcast(E4M3), rhs_scale=hid_scales[:], start=False, stop=True,
+            )
+            result = tile([P, O], F32, "result%d" % h)
+            nc.vector.tensor_tensor(result[:], p_banks[h][:], floors[h][:], MAX)
+            queue.dma_start(out[P * h : P * (h + 1), :], result[:])

@@ -41,58 +41,59 @@ def tile_list_largestpicked_twotab_further_stepfloor_kernel(
             nc.sync.dma_start(t[:], src)
             return t
 
-        def load_plane(engine, plane, scales):
+        def load_plane(queues, plane, scales):
             rows = scales[0].bitcast(I32)
             for q in range(QUADS):
-                engine.dma_start(plane[QROWS * q : QROWS * q + PACK, :].bitcast(I32), rows[PACK * q : PACK * (q + 1), :])
+                queues[q].dma_start(plane[QROWS * q : QROWS * q + PACK, :].bitcast(I32), rows[PACK * q : PACK * (q + 1), :])
+
+        def load_folded(queue, stage, scales):
+            rows = scales[0].bitcast(I32).rearrange("(h q r) c -> q r h c", h=2, q=2)
+            for q in range(2):
+                queue.dma_start(stage[QROWS * q : QROWS * q + PACK, :, :], rows[q])
 
         xt_plane = tile([P, T], U8, "xt_plane")
+        w_stage = tile([P, 2, R // 4], I32, "w_stage")
+        w2_stage = tile([P, 2, R // 4], I32, "w2_stage")
         xo_plane = tile([P, T], U8, "xo_plane")
-        w_plane = tile([P, 2 * R], U8, "w_plane")
-        ws_plane = tile([P, N], U8, "ws_plane")
-        wb_plane = tile([P, N], U8, "wb_plane")
-        for plane in (xt_plane, xo_plane, w_plane, ws_plane, wb_plane):
-            nc.vector.memset(plane[:].bitcast(I32), 0)
+        out_stage = tile([2 * QROWS, 2, 2 * N // 4], I32, "out_stage")
+        nc.vector.memset(xt_plane[:].bitcast(I32), 0)
+        nc.vector.memset(w_stage[:], 0)
+        nc.vector.memset(w2_stage[:], 0)
+        nc.vector.memset(xo_plane[:].bitcast(I32), 0)
+        nc.vector.memset(out_stage[:], 0)
 
-        w_stage = tile([PACK, QUADS, 2 * R // 4], I32, "w_stage")
-        for i, scales in enumerate((w_scales, w2_scales)):
-            nc.sync.dma_start(
-                w_stage[:, :, i * R // 4 : (i + 1) * R // 4],
-                scales[0].bitcast(I32).rearrange("(q r) c -> r q c", r=PACK),
-            )
-        idx = load_list(offs, "idx")
-        load_plane(nc.scalar, xt_plane, xt_scales)
-        xt_tab = tile([P, T], U32, "xt_tab")
-        nc.sync.dma_start(xt_tab[:].bitcast(I32), xt_words[0].rearrange("p c r -> p (c r)").bitcast(I32))
         w_raw = tile([P, R], U16, "w_raw")
-        nc.sync.dma_start(w_raw[:].bitcast(I32), w_words[0].bitcast(I32))
+        nc.gpsimd.dma_start(w_raw[:].bitcast(I32), w_words[0].bitcast(I32))
         w2_raw = tile([P, R], U16, "w2_raw")
-        nc.sync.dma_start(w2_raw[:].bitcast(I32), w2_words[0].bitcast(I32))
-        xo_tab = tile([P, T], U32, "xo_tab")
-        nc.sync.dma_start(xo_tab[:].bitcast(I32), xo_words[0].rearrange("p c r -> p (c r)").bitcast(I32))
-        idx2 = load_list(offs2, "idx2")
-        load_plane(nc.sync, xo_plane, xo_scales)
-        tz_rows = [tile([P, E], F32, "tz_rows%d" % h) for h in range(2)]
-        idx4 = load_list(offs4, "idx4")
-        nc.sync.dma_start(tz_rows[0][:], tz[0:P, :])
-        idx3 = load_list(offs3, "idx3")
-        nc.sync.dma_start(tz_rows[1][:], tz[P : 2 * P, :])
-        idx5 = load_list(offs5, "idx5")
-        load_plane(nc.sync, ws_plane, ws_scales)
-        load_plane(nc.sync, wb_plane, wb_scales)
-
-        sa_cols = tile([P, PACK], F32, "sa_cols")
-        nc.gpsimd.dma_start(sa_cols[:], sa.rearrange("(p t) o -> p (t o)", t=PACK))
-        so_cols = tile([P, 2], F32, "so_cols")
-        with nc.allow_non_contiguous_dma(reason="one step a partition"):
-            nc.gpsimd.dma_start(so_cols[:], so.rearrange("(h p) o -> p (h o)", p=P))
+        nc.gpsimd.dma_start(w2_raw[:].bitcast(I32), w2_words[0].bitcast(I32))
         ws_codes = tile([P, N], U16, "ws_codes")
         nc.gpsimd.dma_start(ws_codes[:].bitcast(I32), ws_words[0].bitcast(I32))
         wb_codes = tile([P, N], U16, "wb_codes")
         nc.gpsimd.dma_start(wb_codes[:].bitcast(I32), wb_words[0].bitcast(I32))
 
-        for q in range(QUADS):
-            nc.vector.tensor_copy(w_plane[QROWS * q : QROWS * q + PACK, :].bitcast(I32), w_stage[:, q, :])
+        idx = load_list(offs, "idx")
+        load_plane((nc.sync, nc.sync, nc.scalar, nc.scalar), xt_plane, xt_scales)
+        load_folded(nc.scalar, w_stage, w_scales)
+        xt_tab = tile([P, T], U32, "xt_tab")
+        nc.sync.dma_start(xt_tab[:].bitcast(I32), xt_words[0].rearrange("p c r -> p (c r)").bitcast(I32))
+        load_folded(nc.sync, w2_stage, w2_scales)
+        xo_tab = tile([P, T], U32, "xo_tab")
+        nc.sync.dma_start(xo_tab[:].bitcast(I32), xo_words[0].rearrange("p c r -> p (c r)").bitcast(I32))
+        idx2 = load_list(offs2, "idx2")
+        load_plane((nc.sync,) * QUADS, xo_plane, xo_scales)
+        idx4 = load_list(offs4, "idx4")
+        tz_rows = [tile([P, E], F32, "tz_rows%d" % h) for h in range(2)]
+        nc.sync.dma_start(tz_rows[0][:], tz[0:P, :])
+        idx3 = load_list(offs3, "idx3")
+        sa_cols = tile([P, PACK], F32, "sa_cols")
+        nc.sync.dma_start(sa_cols[:], sa.rearrange("(p t) o -> p (t o)", t=PACK))
+        load_folded(nc.sync, out_stage[:, :, 0 : N // 4], ws_scales)
+        load_folded(nc.sync, out_stage[:, :, N // 4 : 2 * N // 4], wb_scales)
+        nc.sync.dma_start(tz_rows[1][:], tz[P : 2 * P, :])
+        so_cols = tile([P, 2], F32, "so_cols")
+        with nc.allow_non_contiguous_dma(reason="one step a partition"):
+            nc.sync.dma_start(so_cols[:], so.rearrange("(h p) o -> p (h o)", p=P))
+        idx5 = load_list(offs5, "idx5")
 
         def gather(tab, plane, offsets, count, name):
             scales = tile([P, count], U8, name + "_scales")
@@ -101,16 +102,18 @@ def tile_list_largestpicked_twotab_further_stepfloor_kernel(
             nc.vector.tensor_copy(codes[:], tab[:].indirect(offsets[:]))
             return codes, scales
 
-        def deal(raw, plane, name):
+        def deal(raw, stage, name):
             codes = tile([P, PACK, P], U16, name + "_codes")
             nc.scalar.copy(codes[:], raw[:].rearrange("p (m t) -> p t m", t=PACK))
             scales = tile([P, PACK, P], U8, name + "_scales")
-            nc.vector.tensor_copy(scales[:], plane.rearrange("p (m t) -> p t m", t=PACK))
+            nc.vector.tensor_copy(stage[2 * QROWS : P, 0, :], stage[0 : 2 * QROWS, 1, :])
+            nc.vector.tensor_copy(scales[:], stage[:, 0, :].bitcast(U8).rearrange("p (m t) -> p t m", t=PACK))
             return codes, scales
 
         xa_codes, xa_scales = gather(xt_tab, xt_plane, idx, J, "xa")
-        w_codes, w_sc = deal(w_raw, w_plane[:, 0:R], "w")
-        a_rows = tile([P, PACK, J], F32, "a_rows")
+        w_codes, w_sc = deal(w_raw, w_stage, "w")
+        w2_codes, w2_sc = deal(w2_raw, w2_stage, "w2")
+        a_rows = tile([P, PACK, J], F32, "w2_raw")
         for pair in range(2):
             a_bank = ps.tile([P, 2, J], F32, name="a_bank%d" % pair)
             for u in range(2):
@@ -121,7 +124,6 @@ def tile_list_largestpicked_twotab_further_stepfloor_kernel(
                 )
             nc.scalar.copy(a_rows[:, 2 * pair : 2 * pair + 2, :], a_bank[:])
 
-        w2_codes, w2_sc = deal(w2_raw, w_plane[:, R : 2 * R], "w2")
         xb_codes, xb_scales = gather(xo_tab, xo_plane, idx2, J, "xb")
         xs_codes, xs_scales = gather(xt_tab, xt_plane, idx4, O, "xs")
 
@@ -136,19 +138,20 @@ def tile_list_largestpicked_twotab_further_stepfloor_kernel(
             nc.vector.tensor_tensor(g1[:], b_bank[:], a_rows[:, t, :], MAX)
             nc.scalar.activation(hid[:, t, :], g1[:].indirect(idx3[:]), COPY, scale=sa_cols[:, t : t + 1])
 
+        out_plane = tile([P, 2 * N], U8, "out_plane")
+        for h in range(2):
+            nc.vector.tensor_copy(out_plane[2 * QROWS * h : 2 * QROWS * (h + 1), :].bitcast(I32), out_stage[:, h, :])
         p_banks = [ps.tile([P, O], F32, name="p_bank%d" % h) for h in range(2)]
-        floors = []
+        floors = tile([P, 2, O], F32, "g1_3")
         for h in range(2):
             nc.tensor.matmul_mx(
                 out=p_banks[h][:], lhsT=ws_codes[:, P * h : P * (h + 1)].bitcast(E2M1),
-                lhsT_scale=ws_plane[:, P * h : P * (h + 1)],
+                lhsT_scale=out_plane[:, P * h : P * (h + 1)],
                 rhs=xs_codes[:].bitcast(E5M2), rhs_scale=xs_scales[:], start=True, stop=False,
             )
-            floor = tile([P, O], F32, "floor%d" % h)
-            nc.scalar.activation(floor[:], tz_rows[h][:].indirect(idx5[:]), COPY, scale=so_cols[:, h : h + 1])
-            floors.append(floor)
+            nc.scalar.activation(floors[:, h, :], tz_rows[h][:].indirect(idx5[:]), COPY, scale=so_cols[:, h : h + 1])
 
-        hid_woven = tile([P, O, PACK], BF16, "hid_woven")
+        hid_woven = tile([P, O, PACK], BF16, "out_stage")
         nc.vector.tensor_copy(hid_woven[:], hid[:].rearrange("p t o -> p o t"))
         hid_codes = tile([P, O], U32, "hid_codes")
         hid_scales = tile([P, O], U8, "hid_scales")
@@ -158,9 +161,9 @@ def tile_list_largestpicked_twotab_further_stepfloor_kernel(
         for h, queue in enumerate((nc.sync, nc.scalar)):
             nc.tensor.matmul_mx(
                 out=p_banks[h][:], lhsT=wb_codes[:, P * h : P * (h + 1)].bitcast(E2M1),
-                lhsT_scale=wb_plane[:, P * h : P * (h + 1)],
+                lhsT_scale=out_plane[:, N + P * h : N + P * (h + 1)],
                 rhs=hid_codes[:].bitcast(E4M3), rhs_scale=hid_scales[:], start=False, stop=True,
             )
             result = tile([P, O], F32, "result%d" % h)
-            nc.vector.tensor_tensor(result[:], p_banks[h][:], floors[h][:], MAX)
+            nc.vector.tensor_tensor(result[:], p_banks[h][:], floors[:, h, :], MAX)
             queue.dma_start(out[P * h : P * (h + 1), :], result[:])

@@ -52,31 +52,27 @@ def tile_list_largestpicked_twotab_further_stepfloor_kernel(
                 queue.dma_start(stage[QROWS * q : QROWS * q + PACK, :, :], rows[q])
 
         xt_plane = tile([P, T], U8, "xt_plane")
-        w_stage = tile([P, 2, R // 4], I32, "w_stage")
-        w2_stage = tile([P, 2, R // 4], I32, "w2_stage")
+        w_plane = tile([P, 2 * R], U8, "w_plane")
         xo_plane = tile([P, T], U8, "xo_plane")
         out_stage = tile([2 * QROWS, 2, 2 * N // 4], I32, "out_stage")
-        nc.vector.memset(xt_plane[:].bitcast(I32), 0)
-        nc.vector.memset(w_stage[:], 0)
-        nc.vector.memset(w2_stage[:], 0)
-        nc.vector.memset(xo_plane[:].bitcast(I32), 0)
+        for plane in (xt_plane, w_plane, xo_plane):
+            nc.vector.memset(plane[:].bitcast(I32), 0)
         nc.vector.memset(out_stage[:], 0)
 
-        w_raw = tile([P, R], U16, "w_raw")
-        nc.gpsimd.dma_start(w_raw[:].bitcast(I32), w_words[0].bitcast(I32))
-        w2_raw = tile([P, R], U16, "w2_raw")
-        nc.gpsimd.dma_start(w2_raw[:].bitcast(I32), w2_words[0].bitcast(I32))
-        ws_codes = tile([P, N], U16, "ws_codes")
-        nc.gpsimd.dma_start(ws_codes[:].bitcast(I32), ws_words[0].bitcast(I32))
-        wb_codes = tile([P, N], U16, "wb_codes")
-        nc.gpsimd.dma_start(wb_codes[:].bitcast(I32), wb_words[0].bitcast(I32))
-
+        w_stage = tile([PACK, QUADS, 2 * R // 4], I32, "w_stage")
+        for i, scales in enumerate((w_scales, w2_scales)):
+            nc.scalar.dma_start(
+                w_stage[:, :, i * R // 4 : (i + 1) * R // 4],
+                scales[0].bitcast(I32).rearrange("(q r) c -> r q c", r=PACK),
+            )
         idx = load_list(offs, "idx")
         load_plane((nc.sync, nc.sync, nc.scalar, nc.scalar), xt_plane, xt_scales)
-        load_folded(nc.scalar, w_stage, w_scales)
         xt_tab = tile([P, T], U32, "xt_tab")
         nc.sync.dma_start(xt_tab[:].bitcast(I32), xt_words[0].rearrange("p c r -> p (c r)").bitcast(I32))
-        load_folded(nc.sync, w2_stage, w2_scales)
+        w_raw = tile([P, R], U16, "w_raw")
+        nc.sync.dma_start(w_raw[:].bitcast(I32), w_words[0].bitcast(I32))
+        w2_raw = tile([P, R], U16, "w2_raw")
+        nc.sync.dma_start(w2_raw[:].bitcast(I32), w2_words[0].bitcast(I32))
         xo_tab = tile([P, T], U32, "xo_tab")
         nc.sync.dma_start(xo_tab[:].bitcast(I32), xo_words[0].rearrange("p c r -> p (c r)").bitcast(I32))
         idx2 = load_list(offs2, "idx2")
@@ -90,10 +86,17 @@ def tile_list_largestpicked_twotab_further_stepfloor_kernel(
         load_folded(nc.sync, out_stage[:, :, 0 : N // 4], ws_scales)
         load_folded(nc.sync, out_stage[:, :, N // 4 : 2 * N // 4], wb_scales)
         nc.sync.dma_start(tz_rows[1][:], tz[P : 2 * P, :])
+        idx5 = load_list(offs5, "idx5")
         so_cols = tile([P, 2], F32, "so_cols")
         with nc.allow_non_contiguous_dma(reason="one step a partition"):
             nc.sync.dma_start(so_cols[:], so.rearrange("(h p) o -> p (h o)", p=P))
-        idx5 = load_list(offs5, "idx5")
+        ws_codes = tile([P, N], U16, "ws_codes")
+        nc.sync.dma_start(ws_codes[:].bitcast(I32), ws_words[0].bitcast(I32))
+        wb_codes = tile([P, N], U16, "wb_codes")
+        nc.sync.dma_start(wb_codes[:].bitcast(I32), wb_words[0].bitcast(I32))
+
+        for q in range(QUADS):
+            nc.vector.tensor_copy(w_plane[QROWS * q : QROWS * q + PACK, :].bitcast(I32), w_stage[:, q, :])
 
         def gather(tab, plane, offsets, count, name):
             scales = tile([P, count], U8, name + "_scales")
@@ -102,17 +105,16 @@ def tile_list_largestpicked_twotab_further_stepfloor_kernel(
             nc.vector.tensor_copy(codes[:], tab[:].indirect(offsets[:]))
             return codes, scales
 
-        def deal(raw, stage, name):
+        def deal(raw, plane, name):
             codes = tile([P, PACK, P], U16, name + "_codes")
             nc.scalar.copy(codes[:], raw[:].rearrange("p (m t) -> p t m", t=PACK))
             scales = tile([P, PACK, P], U8, name + "_scales")
-            nc.vector.tensor_copy(stage[2 * QROWS : P, 0, :], stage[0 : 2 * QROWS, 1, :])
-            nc.vector.tensor_copy(scales[:], stage[:, 0, :].bitcast(U8).rearrange("p (m t) -> p t m", t=PACK))
+            nc.vector.tensor_copy(scales[:], plane.rearrange("p (m t) -> p t m", t=PACK))
             return codes, scales
 
         xa_codes, xa_scales = gather(xt_tab, xt_plane, idx, J, "xa")
-        w_codes, w_sc = deal(w_raw, w_stage, "w")
-        w2_codes, w2_sc = deal(w2_raw, w2_stage, "w2")
+        w_codes, w_sc = deal(w_raw, w_plane[:, 0:R], "w")
+        w2_codes, w2_sc = deal(w2_raw, w_plane[:, R : 2 * R], "w2")
         a_rows = tile([P, PACK, J], F32, "w2_raw")
         for pair in range(2):
             a_bank = ps.tile([P, 2, J], F32, name="a_bank%d" % pair)

from contextlib import ExitStack

import concourse.mybir as mybir

K, T, J, R, O, N, E = 512, 1024, 256, 512, 128, 256, 1024
FLOPS = 2 * K * R * J * 2 + 2 * R * N * O * 2

F32 = mybir.dt.float32
BF16 = mybir.dt.bfloat16
I32 = mybir.dt.int32
U32 = mybir.dt.uint32
U16 = mybir.dt.uint16
U8 = mybir.dt.uint8
E4M3 = mybir.dt.float8_e4m3fn_x4
E5M2 = mybir.dt.float8_e5m2_x4
E2M1 = mybir.dt.float4_e2m1fn_x4
COPY = mybir.ActivationFunctionType.Copy
MAX = mybir.AluOpType.max

P = 128
PACK = 4
QUADS = 4
QROWS = 32


def tile_list_largestpicked_twotab_further_stepfloor_kernel(
    tc, xt_words, xt_scales, w_words, w_scales, xo_words, xo_scales, w2_words, w2_scales, sa,
    wb_words, wb_scales, ws_words, ws_scales, tz, so, offs, offs2, offs3, offs4, offs5, out,
):
    nc = tc.nc
    with ExitStack() as ctx:
        lists = ctx.enter_context(tc.tile_pool(name="lists", bufs=1))
        sb = ctx.enter_context(tc.tile_pool(name="sb", bufs=1))
        ps = ctx.enter_context(tc.psum_pool(name="ps", bufs=1))

        def tile(shape, dtype, name):
            return sb.tile(shape, dtype, name=name, align_bytes=64)

        def load_list(src, name):
            t = lists.tile(list(src.shape), U16, name=name)
            nc.sync.dma_start(t[:], src)
            return t

        def load_plane(queues, plane, scales):
            rows = scales[0].bitcast(I32)
            for q in range(QUADS):
                queues[q].dma_start(plane[QROWS * q : QROWS * q + PACK, :].bitcast(I32), rows[PACK * q : PACK * (q + 1), :])

        def load_folded(queue, stage, scales):
            rows = scales[0].bitcast(I32).rearrange("(h q r) c -> q r h c", h=2, q=2)
            for q in range(2):
                queue.dma_start(stage[QROWS * q : QROWS * q + PACK, :, :], rows[q])

        xt_plane = tile([P, T], U8, "xt_plane")
        w_plane = tile([P, 2 * R], U8, "w_plane")
        xo_plane = tile([P, T], U8, "xo_plane")
        out_stage = tile([2 * QROWS, 2, 2 * N // 4], I32, "out_stage")
        for plane in (xt_plane, w_plane, xo_plane):
            nc.vector.memset(plane[:].bitcast(I32), 0)
        nc.vector.memset(out_stage[:], 0)

        w_stage = tile([PACK, QUADS, 2 * R // 4], I32, "w_stage")
        for i, scales in enumerate((w_scales, w2_scales)):
            nc.scalar.dma_start(
                w_stage[:, :, i * R // 4 : (i + 1) * R // 4],
                scales[0].bitcast(I32).rearrange("(q r) c -> r q c", r=PACK),
            )
        idx = load_list(offs, "idx")
        load_plane((nc.sync, nc.sync, nc.scalar, nc.scalar), xt_plane, xt_scales)
        xt_tab = tile([P, T], U32, "xt_tab")
        nc.sync.dma_start(xt_tab[:].bitcast(I32), xt_words[0].rearrange("p c r -> p (c r)").bitcast(I32))
        w_raw = tile([P, R], U16, "w_raw")
        nc.sync.dma_start(w_raw[:].bitcast(I32), w_words[0].bitcast(I32))
        w2_raw = tile([P, R], U16, "w2_raw")
        nc.sync.dma_start(w2_raw[:].bitcast(I32), w2_words[0].bitcast(I32))
        xo_tab = tile([P, T], U32, "xo_tab")
        nc.sync.dma_start(xo_tab[:].bitcast(I32), xo_words[0].rearrange("p c r -> p (c r)").bitcast(I32))
        idx2 = load_list(offs2, "idx2")
        load_plane((nc.sync,) * QUADS, xo_plane, xo_scales)
        idx4 = load_list(offs4, "idx4")
        tz_rows = [tile([P, E], F32, "tz_rows%d" % h) for h in range(2)]
        nc.sync.dma_start(tz_rows[0][:], tz[0:P, :])
        idx3 = load_list(offs3, "idx3")
        sa_cols = tile([P, PACK], F32, "sa_cols")
        nc.sync.dma_start(sa_cols[:], sa.rearrange("(p t) o -> p (t o)", t=PACK))
        load_folded(nc.sync, out_stage[:, :, 0 : N // 4], ws_scales)
        load_folded(nc.sync, out_stage[:, :, N // 4 : 2 * N // 4], wb_scales)
        nc.sync.dma_start(tz_rows[1][:], tz[P : 2 * P, :])
        idx5 = load_list(offs5, "idx5")
        so_cols = tile([P, 2], F32, "so_cols")
        with nc.allow_non_contiguous_dma(reason="one step a partition"):
            nc.sync.dma_start(so_cols[:], so.rearrange("(h p) o -> p (h o)", p=P))
        ws_codes = tile([P, N], U16, "ws_codes")
        nc.sync.dma_start(ws_codes[:].bitcast(I32), ws_words[0].bitcast(I32))
        wb_codes = tile([P, N], U16, "wb_codes")
        nc.sync.dma_start(wb_codes[:].bitcast(I32), wb_words[0].bitcast(I32))

        for q in range(QUADS):
            nc.vector.tensor_copy(w_plane[QROWS * q : QROWS * q + PACK, :].bitcast(I32), w_stage[:, q, :])

        def gather(tab, plane, offsets, count, name):
            scales = tile([P, count], U8, name + "_scales")
            nc.vector.tensor_copy(scales[:], plane[:].indirect(offsets[:]))
            codes = tile([P, count], U32, name + "_codes")
            nc.vector.tensor_copy(codes[:], tab[:].indirect(offsets[:]))
            return codes, scales

        def deal(raw, plane, name):
            codes = tile([P, PACK, P], U16, name + "_codes")
            nc.scalar.copy(codes[:], raw[:].rearrange("p (m t) -> p t m", t=PACK))
            scales = tile([P, PACK, P], U8, name + "_scales")
            nc.vector.tensor_copy(scales[:], plane.rearrange("p (m t) -> p t m", t=PACK))
            return codes, scales

        xa_codes, xa_scales = gather(xt_tab, xt_plane, idx, J, "xa")
        w_codes, w_sc = deal(w_raw, w_plane[:, 0:R], "w")
        w2_codes, w2_sc = deal(w2_raw, w_plane[:, R : 2 * R], "w2")
        a_rows = tile([P, PACK, J], F32, "w2_raw")
        for pair in range(2):
            a_bank = ps.tile([P, 2, J], F32, name="a_bank%d" % pair)
            for u in range(2):
                t = 2 * pair + u
                nc.tensor.matmul_mx(
                    out=a_bank[:, u, :], lhsT=w_codes[:, t, :].bitcast(E2M1), lhsT_scale=w_sc[:, t, :],
                    rhs=xa_codes[:].bitcast(E5M2), rhs_scale=xa_scales[:], start=True, stop=True,
                )
            nc.scalar.copy(a_rows[:, 2 * pair : 2 * pair + 2, :], a_bank[:])

        xb_codes, xb_scales = gather(xo_tab, xo_plane, idx2, J, "xb")
        xs_codes, xs_scales = gather(xt_tab, xt_plane, idx4, O, "xs")

        hid = tile([P, PACK, O], BF16, "hid")
        for t in range(PACK):
            b_bank = ps.tile([P, J], F32, name="b_bank%d" % t)
            nc.tensor.matmul_mx(
                out=b_bank[:], lhsT=w2_codes[:, t, :].bitcast(E2M1), lhsT_scale=w2_sc[:, t, :],
                rhs=xb_codes[:].bitcast(E4M3), rhs_scale=xb_scales[:], start=True, stop=True,
            )
            g1 = tile([P, J], F32, "g1_%d" % t)
            nc.vector.tensor_tensor(g1[:], b_bank[:], a_rows[:, t, :], MAX)
            nc.scalar.activation(hid[:, t, :], g1[:].indirect(idx3[:]), COPY, scale=sa_cols[:, t : t + 1])

        out_plane = tile([P, 2 * N], U8, "out_plane")
        for h in range(2):
            nc.vector.tensor_copy(out_plane[2 * QROWS * h : 2 * QROWS * (h + 1), :].bitcast(I32), out_stage[:, h, :])
        p_banks = [ps.tile([P, O], F32, name="p_bank%d" % h) for h in range(2)]
        floors = tile([P, 2, O], F32, "g1_3")
        for h in range(2):
            nc.tensor.matmul_mx(
                out=p_banks[h][:], lhsT=ws_codes[:, P * h : P * (h + 1)].bitcast(E2M1),
                lhsT_scale=out_plane[:, P * h : P * (h + 1)],
                rhs=xs_codes[:].bitcast(E5M2), rhs_scale=xs_scales[:], start=True, stop=False,
            )
            nc.scalar.activation(floors[:, h, :], tz_rows[h][:].indirect(idx5[:]), COPY, scale=so_cols[:, h : h + 1])

        hid_woven = tile([P, O, PACK], BF16, "out_stage")
        nc.vector.tensor_copy(hid_woven[:], hid[:].rearrange("p t o -> p o t"))
        hid_codes = tile([P, O], U32, "hid_codes")
        hid_scales = tile([P, O], U8, "hid_scales")
        nc.vector.quantize_mx(
            out=hid_codes[:].bitcast(E4M3), scales=hid_scales[:], in_=hid_woven[:].rearrange("p o t -> p (o t)")
        )
        for h, queue in enumerate((nc.sync, nc.scalar)):
            nc.tensor.matmul_mx(
                out=p_banks[h][:], lhsT=wb_codes[:, P * h : P * (h + 1)].bitcast(E2M1),
                lhsT_scale=out_plane[:, N + P * h : N + P * (h + 1)],
                rhs=hid_codes[:].bitcast(E4M3), rhs_scale=hid_scales[:], start=False, stop=True,
            )
            result = tile([P, O], F32, "result%d" % h)
            nc.vector.tensor_tensor(result[:], p_banks[h][:], floors[:, h, :], MAX)
            queue.dma_start(out[P * h : P * (h + 1), :], result[:])
